import numpy as np
import ml_dtypes


def mxq(x, axis, fmt="e4m3"):
    dtype, down = {"e4m3": (ml_dtypes.float8_e4m3fn, 7), "e5m2": (ml_dtypes.float8_e5m2, 14)}[fmt]
    v = np.moveaxis(np.asarray(x, np.float32).astype(ml_dtypes.bfloat16).astype(np.float64), axis, -1)
    blocks = v.reshape(v.shape[:-1] + (-1, 32))
    amax = np.abs(blocks).max(-1, keepdims=True)
    byte = np.maximum(np.where(amax > 0, np.frexp(amax)[1] - 1 + 127, 0) - down, 1)
    scale = np.exp2(byte - 127.0)
    codes = (blocks / scale).astype(np.float32).astype(dtype).astype(np.float64)
    return np.moveaxis((codes * scale).reshape(v.shape), -1, axis)


WIDE = False


def mx_kscale(k):
    if not WIDE:
        return np.ones(k)
    levels = np.array([10, -10, 5, -5, 0])
    if k % 512:
        return np.exp2(np.random.permutation(np.resize(levels, k // 32))).repeat(32)
    a = np.empty((k // 512, 16))
    for p in range(k // 512):
        a[p, :8] = np.random.permutation(np.resize(levels, 8))
        for g in range(8):
            far = levels[np.abs(levels - a[p, g]) >= 10]
            a[p, g + 8] = far[np.random.randint(len(far))]
    return np.exp2(a.ravel()).repeat(32)


def f64(x):
    return np.asarray(x).astype(np.float64)


def striped(idx):
    return np.tile(idx.reshape(-1, 16).T, (8, 1)).astype(np.uint16)


def unstriped(offs):
    return offs[:16].T.reshape(-1).astype(np.int64)


E2M1 = np.array([0.0, 0.5, 1.0, 1.5, 2.0, 3.0, 4.0, 6.0, -0.0, -0.5, -1.0, -1.5, -2.0, -3.0, -4.0, -6.0])


def pack_weight(w, fmt):
    k, n = w.shape
    w = f64(np.asarray(w, np.float32).astype(ml_dtypes.bfloat16)).reshape(k // 32, 32, n)
    amax = np.abs(w).max(1)
    if fmt == "e4m3":
        byte = np.frexp(amax)[1] - 1 + 127 - 7
    else:
        mant, ex = np.frexp(amax / 6.0)
        byte = np.where(mant > 0.5, ex, ex - 1) + 127
    byte = np.clip(np.where(amax > 0, byte, 1), 1, 254)
    scaled = (w * np.exp2(127.0 - byte)[:, None, :]).reshape(k, n).astype(np.float32)
    by_word = np.ascontiguousarray(scaled.reshape(k // 512, 128, 4, n).transpose(0, 1, 3, 2))
    if fmt == "e4m3":
        words = by_word.astype(ml_dtypes.float8_e4m3fn).view(np.uint8)
    else:
        c = by_word.astype(ml_dtypes.float4_e2m1fn).view(np.uint8) & 0xF
        words = (c[..., 0::2] | (c[..., 1::2] << 4)).reshape(k // 512, 128, 2 * n)
    return np.ascontiguousarray(words), np.ascontiguousarray(byte.astype(np.uint8).reshape(k // 512, 16, n))


def unpack_weight(words, scales, fmt):
    g, _, n = scales.shape
    words = np.ascontiguousarray(words).reshape(g, 128, n, -1)
    if fmt == "e4m3":
        vals = words.view(ml_dtypes.float8_e4m3fn).astype(np.float64)
    else:
        nib = np.empty((g, 128, n, 4), np.uint8)
        nib[..., 0::2] = words & 0xF
        nib[..., 1::2] = words >> 4
        vals = E2M1[nib]
    vals = vals * np.repeat(np.exp2(scales.astype(np.float64) - 127.0), 8, axis=1)[..., None]
    return vals.transpose(0, 1, 3, 2).reshape(g * 512, n)


def gelu(v):
    return 0.5 * v * (1.0 + np.tanh(np.sqrt(2.0 / np.pi) * (v + 0.044715 * v**3)))


def often(T, S):
    return np.random.permutation(T)[(T * np.random.uniform(0, 1, S) ** 4).astype(np.int64)]


K, H, N, T, S, T2, P = 1024, 1024, 512, 2048, 1024, 2048, 512

def setup_inputs():
    n = np.random.standard_normal
    s = mx_kscale(K)[:, None]
    u = mx_kscale(H)[:, None]
    tab_words, tab_scales = pack_weight(n((K, T)) * s, "e4m3")
    tab2_words, tab2_scales = pack_weight(n((K, T2)) * s, "e4m3")
    wd_words, wd_scales = pack_weight(n((H, N)) / np.sqrt(H) / u, "e2m1")
    return {
        "tab_words": tab_words, "tab_scales": tab_scales,
        "tab2_words": tab2_words, "tab2_scales": tab2_scales,
        "offs": striped(np.random.permutation(T)[:S]),
        "pos1": striped(often(S, P)),
        "offs2": striped(np.random.permutation(T2)[:P]),
        "w1": (n((K, H)) / np.sqrt(K) / s * u.T).astype(np.float32),
        "ge": (np.exp(0.3 * n(H)) / u[:, 0]).astype(np.float32),
        "wd_words": wd_words, "wd_scales": wd_scales,
        "wm": (n((H, N)) / np.sqrt(H) / u).astype(np.float32),
        "bo": (0.5 * n(N)).astype(np.float32),
    }

def reference(tab_words, tab_scales, tab2_words, tab2_scales, offs, pos1, offs2, w1, ge, wd_words, wd_scales, wm, bo):
    v = unpack_weight(tab_words, tab_scales, "e4m3")[:, unstriped(offs)]
    v2 = unpack_weight(tab2_words, tab2_scales, "e4m3")[:, unstriped(offs2)]
    w1q = mxq(f64(w1), 0, "e4m3")
    h = w1q.T @ v
    b = w1q.T @ v2
    a = h[:, unstriped(pos1)]
    d = np.abs(a - b)
    e = f64(ge)[:, None] * a * b
    dq = mxq(d, 0, "e4m3")
    eq = mxq(e, 0, "e4m3")
    wd = unpack_weight(wd_words, wd_scales, "e2m1")
    wmq = mxq(f64(wm), 0, "e4m3")
    y = wd.T @ dq + wmq.T @ eq
    return y + f64(bo)[:, None]

@@ -1,0 +1,323 @@
+from contextlib import ExitStack
+
+import concourse.mybir as mybir
+
+K, H, N, T, S, M = 1024, 1024, 512, 2048, 1024, 512
+FLOPS = 2 * K * H * (S + M) + 4 * H * N * M
+
+F32 = mybir.dt.float32
+BF16 = mybir.dt.bfloat16
+I32 = mybir.dt.int32
+U32 = mybir.dt.uint32
+U16 = mybir.dt.uint16
+U8 = mybir.dt.uint8
+FP8X4 = mybir.dt.float8_e4m3fn_x4
+FP4X4 = mybir.dt.float4_e2m1fn_x4
+ACT = mybir.ActivationFunctionType
+ALU = mybir.AluOpType
+
+P = 128
+PACK = 4
+PASS = 512
+BANK = 512
+QUARTER = 128
+
+
+def tile_list_permission_drift_features_kernel(
+    tc, tab_words, tab_scales, tab2_words, tab2_scales, offs, pos1, offs2, w1, ge, wd_words, wd_scales, wm, bo, out
+):
+    nc = tc.nc
+    with ExitStack() as ctx:
+        lists = ctx.enter_context(tc.tile_pool(name="lists", bufs=1))
+        keep = ctx.enter_context(tc.tile_pool(name="keep", bufs=1))
+        psum = ctx.enter_context(tc.psum_pool(name="psum", bufs=1))
+
+        def tile(shape, dtype, name, slot=None):
+            return keep.tile(shape, dtype, name=name, tag=slot or name, align_bytes=64)
+
+        def bank(index, shape, name):
+            return psum.tile(shape, F32, name=name, tag="bank%d" % index)
+
+        offs_t = lists.tile([P, S // 16], U16, name="offs_t")
+        offs2_t = lists.tile([P, M // 16], U16, name="offs2_t")
+        pos1_t = lists.tile([P, M // 16], U16, name="pos1_t")
+
+        tab_s = tile([P, T], U8, "tab_s")
+        tab2_s = tile([P, T], U8, "tab2_s")
+        wd_s = tile([P, 2, N], U8, "wd_s")
+        nc.vector.memset(tab_s[:].bitcast(I32), 0)
+        nc.gpsimd.memset(tab2_s[:].bitcast(I32), 0)
+        nc.gpsimd.memset(wd_s[:].bitcast(I32), 0)
+
+        def load_words(queue, words, a, name):
+            t = tile([P, T], I32, name)
+            queue.dma_start(t[:], words[a].rearrange("p t i -> p (t i)").bitcast(I32))
+            return t
+
+        def load_table_scales(queue, plane, scales):
+            for q in range(4):
+                queue.dma_start(plane[32 * q : 32 * q + 8, :].bitcast(I32), scales[:, 4 * q : 4 * q + 4, :].bitcast(I32))
+
+        def load_rows(src, a, c0, width, name):
+            t = tile([P, PACK, width], F32, name)
+            nc.sync.dma_start(t[:], src[PASS * a : PASS * (a + 1), c0 : c0 + width].rearrange("(p j) c -> p j c", j=PACK))
+            return t
+
+        tab_w = [None, None]
+        nc.sync.dma_start(offs_t[:], offs)
+        tab_w[0] = load_words(nc.sync, tab_words, 0, "tab_w0")
+        nc.sync.dma_start(offs2_t[:], offs2)
+        nc.sync.dma_start(pos1_t[:], pos1)
+        load_table_scales(nc.sync, tab_s, tab_scales)
+        w1_raw = {}
+        w1_raw[0, 0] = [load_rows(w1, 0, 0, 512, "w1_raw00")]
+        tab_w[1] = load_words(nc.sync, tab_words, 1, "tab_w1")
+        w1_raw[0, 1] = [load_rows(w1, 1, 256 * hh, 256, "w1_raw01%d" % hh) for hh in range(2)]
+        tab2_w = [None, None]
+        tab2_w[0] = load_words(nc.sync, tab2_words, 0, "tab2_w0")
+        load_table_scales(nc.sync, tab2_s, tab2_scales)
+        tab2_w[1] = load_words(nc.sync, tab2_words, 1, "tab2_w1")
+        ge_t = tile([P, 2, PACK], F32, "ge_t")
+        nc.sync.dma_start(ge_t[:], ge.rearrange("(g p t) -> p g t", g=2, t=PACK))
+        w1_raw[1, 0] = [load_rows(w1, 0, 512, 512, "w1_raw10")]
+        w1_raw[1, 1] = [load_rows(w1, 1, 512, 512, "w1_raw11")]
+        wm_raw = [load_rows(wm, a, 0, 512, "wm_raw%d" % a) for a in range(2)]
+        wd_w = tile([P, 2, 2 * N], U8, "wd_w")
+        nc.sync.dma_start(wd_w[:].bitcast(I32), wd_words.rearrange("a p c -> p a c").bitcast(I32))
+        for q in range(4):
+            nc.sync.dma_start(
+                wd_s[32 * q : 32 * q + 4, :, :].bitcast(I32),
+                wd_scales[:, 4 * q : 4 * q + 4, :].rearrange("a r n -> r a n").bitcast(I32),
+            )
+        bo_t = tile([P, 4], F32, "bo_t")
+        with nc.allow_non_contiguous_dma(reason="one bias value to a partition"):
+            nc.sync.dma_start(bo_t[:], bo.rearrange("(c p) -> p c", p=P))
+
+        def gather(window, offsets, count, dtype, name, slot=None):
+            t = tile([P, count], dtype, name, slot)
+            nc.vector.tensor_copy(t[:], window.indirect(offsets))
+            return t
+
+        def quantize(src, width, name):
+            codes = tile([P, width], U32, name + "_c")
+            scales = tile([P, width], U8, name + "_s")
+            nc.vector.quantize_mx(out=codes[:].bitcast(FP8X4), scales=scales[:], in_=src)
+            return codes, scales
+
+        w1_bf = {}
+        w1_q = {}
+
+        def round_w1(g, a):
+            w1_bf[g, a] = tile([P, PACK, P, PACK], BF16, "w1_bf%d%d" % (g, a))
+            pieces = w1_raw[g, a]
+            per = P // len(pieces)
+            for i, raw in enumerate(pieces):
+                nc.scalar.copy(
+                    w1_bf[g, a][:, :, per * i : per * (i + 1), :].rearrange("p t m j -> p m j t"),
+                    raw[:].rearrange("p j (m t) -> p m j t", t=PACK),
+                )
+
+        def quantize_w1(g, a):
+            w1_q[g, a] = quantize(w1_bf[g, a][:].rearrange("p t m j -> p (t m j)"), PASS, "w1_q%d%d" % (g, a))
+
+        v_w = [None, None]
+        v_s = gather(tab_s[:], offs_t[:], S, U8, "v_s")
+        v_w[0] = gather(tab_w[0][:].bitcast(U32), offs_t[:], S, U32, "v_w0")
+        round_w1(0, 0)
+        v_w[1] = gather(tab_w[1][:].bitcast(U32), offs_t[:], S, U32, "v_w1")
+        quantize_w1(0, 0)
+        round_w1(0, 1)
+        quantize_w1(0, 1)
+        v2_w = [None, None]
+        v2_w[0] = gather(tab2_w[0][:].bitcast(U32), offs2_t[:], M, U32, "v2_w0")
+        v2_s = gather(tab2_s[:], offs2_t[:], M, U8, "v2_s")
+        v2_w[1] = gather(tab2_w[1][:].bitcast(U32), offs2_t[:], M, U32, "v2_w1")
+
+        def project(dst, g, t, words, plane, cols):
+            for a in range(2):
+                codes, scales = w1_q[g, a]
+                nc.tensor.matmul_mx(
+                    out=dst,
+                    lhsT=codes[:, P * t : P * (t + 1)].bitcast(FP8X4),
+                    lhsT_scale=scales[:, P * t : P * (t + 1)],
+                    rhs=words[a][:, cols].bitcast(FP8X4),
+                    rhs_scale=plane[4 * a : P, cols],
+                    start=(a == 0),
+                    stop=(a == 1),
+                )
+
+        h = {}
+        b = {}
+
+        def make_h(g, t):
+            h[g, t] = tile([P, S], F32, "h%d%d" % (g, t))
+            for half in range(2):
+                cols = slice(BANK * half, BANK * (half + 1))
+                acc = bank((2 * t + half) % 4, [P, BANK], "h_acc%d%d%d" % (g, t, half))
+                project(acc[:], g, t, v_w, v_s, cols)
+                nc.scalar.copy(h[g, t][:, cols], acc[:])
+
+        def make_b(g, t):
+            b[g, t] = bank(4 + t, [P, M], "b_acc%d%d" % (g, t))
+            project(b[g, t][:], g, t, v2_w, v2_s, slice(0, M))
+
+        b_late = {}
+
+        def make_b_late(half):
+            b_late[half] = bank(6 + half, [P, 2, M // 2], "b_late%d" % half)
+            for i in range(2):
+                project(b_late[half][:, i, :], 1, 2 + i, v2_w, v2_s, slice(256 * half, 256 * (half + 1)))
+
+        diff = [tile([P, 4, PACK, QUARTER], BF16, "diff%d" % g) for g in range(2)]
+        prod = [tile([P, 4, PACK, QUARTER], BF16, "prod%d" % g) for g in range(2)]
+        a_t = {}
+
+        def fetch(g, t, slot=None):
+            a_t[g, t] = gather(h[g, t][:], pos1_t[:], M, F32, "a%d%d" % (g, t), slot)
+
+        def combine(g, t):
+            a_q = a_t[g, t][:].rearrange("p (q m) -> p q m", q=4)
+            b_q = b[g, t][:].rearrange("p (q m) -> p q m", q=4)
+            nc.vector.tensor_tensor(diff[g][:, :, t, :], a_q, b_q, ALU.subtract)
+            nc.vector.scalar_tensor_tensor(prod[g][:, :, t, :], b_q, ge_t[:, g, t : t + 1], a_q, ALU.mult, ALU.mult)
+
+        a_late = {}
+
+        def fetch_late(q0, nq, slot):
+            a_late[q0] = tile([P, 2, nq * QUARTER], F32, "a_late%d" % q0, slot)
+            offsets = pos1_t[:, q0 * QUARTER // 16 : (q0 + nq) * QUARTER // 16]
+            for i in range(2):
+                nc.vector.tensor_copy(a_late[q0][:, i, :], h[1, 2 + i][:].indirect(offsets))
+
+        def combine_late(q0, nq):
+            c0 = (q0 % 2) * QUARTER
+            a_q = a_late[q0][:].rearrange("p t (q m) -> p t q m", q=nq)
+            b_q = b_late[q0 // 2][:, :, c0 : c0 + nq * QUARTER].rearrange("p t (q m) -> p t q m", q=nq)
+            nc.vector.tensor_tensor(diff[1][:, q0 : q0 + nq, 2:4, :].rearrange("p q t m -> p t q m"), a_q, b_q, ALU.subtract)
+            for i in range(2):
+                nc.vector.scalar_tensor_tensor(
+                    prod[1][:, q0 : q0 + nq, 2 + i, :], b_q[:, i], ge_t[:, 1, 2 + i : 3 + i], a_q[:, i], ALU.mult, ALU.mult
+                )
+
+        d_bf, e_bf, d_q, e_q = {}, {}, {}, {}
+
+        def weave(tiles, src, name, g, q0, nq, slot, op):
+            tiles[g, q0] = tile([P, nq, QUARTER, PACK], BF16, "%s%d_%d" % (name, g, q0), slot)
+            for q in range(nq):
+                op(
+                    tiles[g, q0][:, q].rearrange("p (c i) t -> p c t i", i=4),
+                    src[g][:, q0 + q].rearrange("p t (c i) -> p c t i", i=4),
+                )
+
+        def weave_d(g, q0, nq, slot=None):
+            weave(d_bf, diff, "d_bf", g, q0, nq, slot, lambda o, i: nc.scalar.activation(o, i, ACT.Abs))
+
+        def weave_e(g, q0, nq, copy, slot=None):
+            weave(e_bf, prod, "e_bf", g, q0, nq, slot, copy)
+
+        def quantize_d(g, q0, nq):
+            d_q[g, q0] = quantize(d_bf[g, q0][:].rearrange("p q m t -> p (q m t)"), nq * QUARTER, "d_q%d_%d" % (g, q0))
+
+        def quantize_e(g, q0, nq):
+            e_q[g, q0] = quantize(e_bf[g, q0][:].rearrange("p q m t -> p (q m t)"), nq * QUARTER, "e_q%d_%d" % (g, q0))
+
+        wm_bf = {}
+        wm_q = {}
+
+        def round_wm(a, slot):
+            wm_bf[a] = tile([P, N, PACK], BF16, "wm_bf%d" % a, slot)
+            nc.scalar.copy(
+                wm_bf[a][:].rearrange("p (c i) j -> p c j i", i=4), wm_raw[a][:].rearrange("p j (c i) -> p c j i", i=4)
+            )
+
+        def quantize_wm(a):
+            wm_q[a] = quantize(wm_bf[a][:].rearrange("p n j -> p (n j)"), N, "wm_q%d" % a)
+
+        y = {}
+
+        def second_stage(g, q0, q):
+            cols = slice(QUARTER * (q - q0), QUARTER * (q - q0 + 1))
+            if g == 0:
+                y[q] = bank(q, [P, 4, QUARTER], "y_acc%d" % q)
+            for c in range(4):
+                nc.tensor.matmul_mx(
+                    out=y[q][:, c, :],
+                    lhsT=wm_q[g][0][:, P * c : P * (c + 1)].bitcast(FP8X4),
+                    lhsT_scale=wm_q[g][1][:, P * c : P * (c + 1)],
+                    rhs=e_q[g, q0][0][:, cols].bitcast(FP8X4),
+                    rhs_scale=e_q[g, q0][1][:, cols],
+                    start=(g == 0 and c == 0),
+                    stop=False,
+                )
+            for c in range(4):
+                nc.tensor.matmul_mx(
+                    out=y[q][:, c, :],
+                    lhsT=wd_w[:, g, 2 * P * c : 2 * P * (c + 1)].bitcast(FP4X4),
+                    lhsT_scale=wd_s[:, g, P * c : P * (c + 1)],
+                    rhs=d_q[g, q0][0][:, cols].bitcast(FP8X4),
+                    rhs_scale=d_q[g, q0][1][:, cols],
+                    start=False,
+                    stop=(g == 1 and c == 3),
+                )
+
+        out_v = out.rearrange("(c p) m -> p c m", p=P)
+
+        def finish(q):
+            res = tile([P, 4, QUARTER], F32, "res%d" % q)
+            if q < 3:
+                for c in range(4):
+                    nc.scalar.activation(res[:, c, :], y[q][:, c, :], ACT.Identity, bias=bo_t[:, c : c + 1])
+            else:
+                nc.vector.tensor_tensor(res[:], y[q][:], bo_t[:].unsqueeze(2).to_broadcast([P, 4, QUARTER]), ALU.add)
+            nc.sync.dma_start(out_v[:, :, QUARTER * q : QUARTER * (q + 1)], res[:])
+
+        for t in range(4):
+            make_h(0, t)
+        for t in range(4):
+            make_b(0, t)
+        round_w1(1, 0)
+        round_w1(1, 1)
+        fetch(0, 0)
+        fetch(0, 1)
+        combine(0, 0)
+        quantize_w1(1, 0)
+        fetch(0, 2)
+        combine(0, 1)
+        quantize_w1(1, 1)
+        fetch(0, 3, "w1_bf11")
+        combine(0, 2)
+        combine(0, 3)
+        round_wm(0, "w1_bf00")
+        make_h(1, 0)
+        make_h(1, 1)
+        make_b(1, 0)
+        make_h(1, 2)
+        make_h(1, 3)
+        make_b(1, 1)
+        make_b_late(0)
+        make_b_late(1)
+        weave_d(0, 0, 4, "w1_q11_c")
+        weave_e(0, 0, 4, nc.scalar.copy, "w1_q10_c")
+        round_wm(1, "w1_bf01")
+        quantize_wm(0)
+        quantize_d(0, 0, 4)
+        quantize_e(0, 0, 4)
+        for q in range(4):
+            second_stage(0, 0, q)
+        quantize_wm(1)
+        fetch(1, 0)
+        fetch(1, 1)
+        combine(1, 0)
+        combine(1, 1)
+        late = [(0, 2, None), (2, 1, "w1_q10_c"), (3, 1, "w1_q10_c")]
+        for q0, nq, slot in late:
+            fetch_late(q0, nq, slot)
+            combine_late(q0, nq)
+            weave_d(1, q0, nq)
+            weave_e(1, q0, nq, nc.vector.tensor_copy if q0 == 3 else nc.scalar.copy)
+            quantize_e(1, q0, nq)
+            quantize_d(1, q0, nq)
+        for q0, nq, slot in late:
+            for q in range(q0, q0 + nq):
+                second_stage(1, q0, q)
+                finish(q)

@@ -33,7 +33,7 @@ def tile_list_permission_drift_features_kernel(
         psum = ctx.enter_context(tc.psum_pool(name="psum", bufs=1))
 
         def tile(shape, dtype, name, slot=None):
-            return keep.tile(shape, dtype, name=name, tag=slot or name, align_bytes=64)
+            return keep.tile(shape, dtype, name=name, tag=slot or name, align_bytes=256)
 
         def bank(index, shape, name):
             return psum.tile(shape, F32, name=name, tag="bank%d" % index)
@@ -74,11 +74,11 @@ def tile_list_permission_drift_features_kernel(
         tab_w[1] = load_words(nc.sync, tab_words, 1, "tab_w1")
         w1_raw[0, 1] = [load_rows(w1, 1, 256 * hh, 256, "w1_raw01%d" % hh) for hh in range(2)]
         tab2_w = [None, None]
-        tab2_w[0] = load_words(nc.sync, tab2_words, 0, "tab2_w0")
         load_table_scales(nc.sync, tab2_s, tab2_scales)
-        tab2_w[1] = load_words(nc.sync, tab2_words, 1, "tab2_w1")
+        tab2_w[0] = load_words(nc.sync, tab2_words, 0, "tab2_w0")
         ge_t = tile([P, 2, PACK], F32, "ge_t")
         nc.sync.dma_start(ge_t[:], ge.rearrange("(g p t) -> p g t", g=2, t=PACK))
+        tab2_w[1] = load_words(nc.sync, tab2_words, 1, "tab2_w1")
         w1_raw[1, 0] = [load_rows(w1, 0, 512, 512, "w1_raw10")]
         w1_raw[1, 1] = [load_rows(w1, 1, 512, 512, "w1_raw11")]
         wm_raw = [load_rows(wm, a, 0, 512, "wm_raw%d" % a) for a in range(2)]
@@ -107,12 +107,12 @@ def tile_list_permission_drift_features_kernel(
         w1_bf = {}
         w1_q = {}
 
-        def round_w1(g, a):
+        def round_w1(g, a, copy):
             w1_bf[g, a] = tile([P, PACK, P, PACK], BF16, "w1_bf%d%d" % (g, a))
             pieces = w1_raw[g, a]
             per = P // len(pieces)
             for i, raw in enumerate(pieces):
-                nc.scalar.copy(
+                copy(
                     w1_bf[g, a][:, :, per * i : per * (i + 1), :].rearrange("p t m j -> p m j t"),
                     raw[:].rearrange("p j (m t) -> p m j t", t=PACK),
                 )
@@ -123,10 +123,10 @@ def tile_list_permission_drift_features_kernel(
         v_w = [None, None]
         v_s = gather(tab_s[:], offs_t[:], S, U8, "v_s")
         v_w[0] = gather(tab_w[0][:].bitcast(U32), offs_t[:], S, U32, "v_w0")
-        round_w1(0, 0)
+        round_w1(0, 0, nc.scalar.copy)
         v_w[1] = gather(tab_w[1][:].bitcast(U32), offs_t[:], S, U32, "v_w1")
         quantize_w1(0, 0)
-        round_w1(0, 1)
+        round_w1(0, 1, nc.scalar.copy)
         quantize_w1(0, 1)
         v2_w = [None, None]
         v2_w[0] = gather(tab2_w[0][:].bitcast(U32), offs2_t[:], M, U32, "v2_w0")
@@ -172,11 +172,17 @@ def tile_list_permission_drift_features_kernel(
         prod = [tile([P, 4, PACK, QUARTER], BF16, "prod%d" % g) for g in range(2)]
         a_t = {}
 
-        def fetch(g, t, slot=None):
-            a_t[g, t] = gather(h[g, t][:], pos1_t[:], M, F32, "a%d%d" % (g, t), slot)
+        def fetch(g, t):
+            a_t[g, t] = gather(h[g, t][:], pos1_t[:], M, F32, "a%d%d" % (g, t))[:]
+
+        def fetch_pair(slot):
+            pair = tile([P, 2, M], F32, "a0_pair", slot)
+            for i in range(2):
+                nc.vector.tensor_copy(pair[:, i, :], h[0, 2 + i][:].indirect(pos1_t[:]))
+                a_t[0, 2 + i] = pair[:, i, :]
 
         def combine(g, t):
-            a_q = a_t[g, t][:].rearrange("p (q m) -> p q m", q=4)
+            a_q = a_t[g, t].rearrange("p (q m) -> p q m", q=4)
             b_q = b[g, t][:].rearrange("p (q m) -> p q m", q=4)
             nc.vector.tensor_tensor(diff[g][:, :, t, :], a_q, b_q, ALU.subtract)
             nc.vector.scalar_tensor_tensor(prod[g][:, :, t, :], b_q, ge_t[:, g, t : t + 1], a_q, ALU.mult, ALU.mult)
@@ -224,9 +230,9 @@ def tile_list_permission_drift_features_kernel(
         wm_bf = {}
         wm_q = {}
 
-        def round_wm(a, slot):
+        def round_wm(a, slot, copy):
             wm_bf[a] = tile([P, N, PACK], BF16, "wm_bf%d" % a, slot)
-            nc.scalar.copy(
+            copy(
                 wm_bf[a][:].rearrange("p (c i) j -> p c j i", i=4), wm_raw[a][:].rearrange("p j (c i) -> p c j i", i=4)
             )
 
@@ -239,32 +245,26 @@ def tile_list_permission_drift_features_kernel(
             cols = slice(QUARTER * (q - q0), QUARTER * (q - q0 + 1))
             if g == 0:
                 y[q] = bank(q, [P, 4, QUARTER], "y_acc%d" % q)
-            for c in range(4):
-                nc.tensor.matmul_mx(
-                    out=y[q][:, c, :],
-                    lhsT=wm_q[g][0][:, P * c : P * (c + 1)].bitcast(FP8X4),
-                    lhsT_scale=wm_q[g][1][:, P * c : P * (c + 1)],
-                    rhs=e_q[g, q0][0][:, cols].bitcast(FP8X4),
-                    rhs_scale=e_q[g, q0][1][:, cols],
-                    start=(g == 0 and c == 0),
-                    stop=False,
-                )
-            for c in range(4):
-                nc.tensor.matmul_mx(
-                    out=y[q][:, c, :],
-                    lhsT=wd_w[:, g, 2 * P * c : 2 * P * (c + 1)].bitcast(FP4X4),
-                    lhsT_scale=wd_s[:, g, P * c : P * (c + 1)],
-                    rhs=d_q[g, q0][0][:, cols].bitcast(FP8X4),
-                    rhs_scale=d_q[g, q0][1][:, cols],
-                    start=False,
-                    stop=(g == 1 and c == 3),
-                )
+            d_part = (wd_w[:, g, :], 2, FP4X4, wd_s[:, g, :], d_q[g, q0])
+            e_part = (wm_q[g][0][:], 1, FP8X4, wm_q[g][1][:], e_q[g, q0])
+            parts = [d_part, e_part] if g == 0 else [e_part, d_part]
+            for i, (words, per, fmt, plane, (codes, scales)) in enumerate(parts):
+                for c in range(4):
+                    nc.tensor.matmul_mx(
+                        out=y[q][:, c, :],
+                        lhsT=words[:, per * P * c : per * P * (c + 1)].bitcast(fmt),
+                        lhsT_scale=plane[:, P * c : P * (c + 1)],
+                        rhs=codes[:, cols].bitcast(FP8X4),
+                        rhs_scale=scales[:, cols],
+                        start=(g == 0 and i == 0 and c == 0),
+                        stop=(g == 1 and i == 1 and c == 3),
+                    )
 
         out_v = out.rearrange("(c p) m -> p c m", p=P)
 
         def finish(q):
             res = tile([P, 4, QUARTER], F32, "res%d" % q)
-            if q < 3:
+            if q < 2:
                 for c in range(4):
                     nc.scalar.activation(res[:, c, :], y[q][:, c, :], ACT.Identity, bias=bo_t[:, c : c + 1])
             else:
@@ -275,19 +275,18 @@ def tile_list_permission_drift_features_kernel(
             make_h(0, t)
         for t in range(4):
             make_b(0, t)
-        round_w1(1, 0)
-        round_w1(1, 1)
+        round_w1(1, 0, nc.vector.tensor_copy)
+        round_w1(1, 1, nc.scalar.copy)
         fetch(0, 0)
         fetch(0, 1)
         combine(0, 0)
         quantize_w1(1, 0)
-        fetch(0, 2)
         combine(0, 1)
         quantize_w1(1, 1)
-        fetch(0, 3, "w1_bf11")
+        fetch_pair("w1_bf11")
         combine(0, 2)
         combine(0, 3)
-        round_wm(0, "w1_bf00")
+        round_wm(0, "w1_bf00", nc.scalar.copy)
         make_h(1, 0)
         make_h(1, 1)
         make_b(1, 0)
@@ -298,7 +297,7 @@ def tile_list_permission_drift_features_kernel(
         make_b_late(1)
         weave_d(0, 0, 4, "w1_q11_c")
         weave_e(0, 0, 4, nc.scalar.copy, "w1_q10_c")
-        round_wm(1, "w1_bf01")
+        round_wm(1, "w1_bf01", nc.scalar.copy)
         quantize_wm(0)
         quantize_d(0, 0, 4)
         quantize_e(0, 0, 4)

@@ -169,23 +169,50 @@ def tile_list_permission_drift_features_kernel(
                 project(b_late[half][:, i, :], 1, 2 + i, v2_w, v2_s, slice(256 * half, 256 * (half + 1)))
 
         diff = [tile([P, 4, PACK, QUARTER], BF16, "diff%d" % g) for g in range(2)]
-        prod = [tile([P, 4, PACK, QUARTER], BF16, "prod%d" % g) for g in range(2)]
-        a_t = {}
+        e_bf = [tile([P, M, PACK], BF16, "e_bf%d" % g) for g in range(2)]
+        a_pair, bg_pair = {}, {}
 
-        def fetch(g, t):
-            a_t[g, t] = gather(h[g, t][:], pos1_t[:], M, F32, "a%d%d" % (g, t))[:]
-
-        def fetch_pair(slot):
-            pair = tile([P, 2, M], F32, "a0_pair", slot)
+        def fetch_pair(g, tp, slot=None):
+            a_pair[g, tp] = tile([P, 2, M], F32, "a%d%d" % (g, tp), slot)
             for i in range(2):
-                nc.vector.tensor_copy(pair[:, i, :], h[0, 2 + i][:].indirect(pos1_t[:]))
-                a_t[0, 2 + i] = pair[:, i, :]
+                nc.vector.tensor_copy(a_pair[g, tp][:, i, :], h[g, 2 * tp + i][:].indirect(pos1_t[:]))
 
-        def combine(g, t):
-            a_q = a_t[g, t].rearrange("p (q m) -> p q m", q=4)
-            b_q = b[g, t][:].rearrange("p (q m) -> p q m", q=4)
-            nc.vector.tensor_tensor(diff[g][:, :, t, :], a_q, b_q, ALU.subtract)
-            nc.vector.scalar_tensor_tensor(prod[g][:, :, t, :], b_q, ge_t[:, g, t : t + 1], a_q, ALU.mult, ALU.mult)
+        def scale_b(g, tp):
+            for i in range(2):
+                t = 2 * tp + i
+                nc.scalar.activation(bg_pair[g, tp][:, i, :], b[g, t][:], ACT.Copy, scale=ge_t[:, g, t : t + 1])
+
+        def scale_b_late():
+            for half in range(2):
+                for i in range(2):
+                    nc.scalar.activation(
+                        bg_pair[1, 1][:, i, 256 * half : 256 * (half + 1)],
+                        b_late[half][:, i, :],
+                        ACT.Copy,
+                        scale=ge_t[:, 1, 2 + i : 3 + i],
+                    )
+
+        def subtract_pair(g, tp):
+            for i in range(2):
+                t = 2 * tp + i
+                nc.vector.tensor_tensor(
+                    diff[g][:, :, t, :],
+                    a_pair[g, tp][:, i, :].rearrange("p (q m) -> p q m", q=4),
+                    b[g, t][:].rearrange("p (q m) -> p q m", q=4),
+                    ALU.subtract,
+                )
+
+        def multiply(g, tp, a_cols, m0, width):
+            nc.gpsimd.tensor_tensor(
+                e_bf[g][:, m0 : m0 + width, 2 * tp : 2 * tp + 2],
+                a_cols.rearrange("p t m -> p m t"),
+                bg_pair[g, tp][:, :, m0 : m0 + width].rearrange("p t m -> p m t"),
+                ALU.mult,
+            )
+
+        def multiply_pair(g, tp):
+            for half in range(2):
+                multiply(g, tp, a_pair[g, tp][:, :, 256 * half : 256 * (half + 1)], 256 * half, 256)
 
         a_late = {}
 
@@ -200,32 +227,25 @@ def tile_list_permission_drift_features_kernel(
             a_q = a_late[q0][:].rearrange("p t (q m) -> p t q m", q=nq)
             b_q = b_late[q0 // 2][:, :, c0 : c0 + nq * QUARTER].rearrange("p t (q m) -> p t q m", q=nq)
             nc.vector.tensor_tensor(diff[1][:, q0 : q0 + nq, 2:4, :].rearrange("p q t m -> p t q m"), a_q, b_q, ALU.subtract)
-            for i in range(2):
-                nc.vector.scalar_tensor_tensor(
-                    prod[1][:, q0 : q0 + nq, 2 + i, :], b_q[:, i], ge_t[:, 1, 2 + i : 3 + i], a_q[:, i], ALU.mult, ALU.mult
-                )
+            multiply(1, 1, a_late[q0][:], q0 * QUARTER, nq * QUARTER)
 
-        d_bf, e_bf, d_q, e_q = {}, {}, {}, {}
-
-        def weave(tiles, src, name, g, q0, nq, slot, op):
-            tiles[g, q0] = tile([P, nq, QUARTER, PACK], BF16, "%s%d_%d" % (name, g, q0), slot)
-            for q in range(nq):
-                op(
-                    tiles[g, q0][:, q].rearrange("p (c i) t -> p c t i", i=4),
-                    src[g][:, q0 + q].rearrange("p t (c i) -> p c t i", i=4),
-                )
+        d_bf, d_q, e_q = {}, {}, {}
 
         def weave_d(g, q0, nq, slot=None):
-            weave(d_bf, diff, "d_bf", g, q0, nq, slot, lambda o, i: nc.scalar.activation(o, i, ACT.Abs))
-
-        def weave_e(g, q0, nq, copy, slot=None):
-            weave(e_bf, prod, "e_bf", g, q0, nq, slot, copy)
+            d_bf[g, q0] = tile([P, nq, QUARTER, PACK], BF16, "d_bf%d_%d" % (g, q0), slot)
+            for q in range(nq):
+                nc.scalar.activation(
+                    d_bf[g, q0][:, q].rearrange("p (c i) t -> p c t i", i=4),
+                    diff[g][:, q0 + q].rearrange("p t (c i) -> p c t i", i=4),
+                    ACT.Abs,
+                )
 
         def quantize_d(g, q0, nq):
             d_q[g, q0] = quantize(d_bf[g, q0][:].rearrange("p q m t -> p (q m t)"), nq * QUARTER, "d_q%d_%d" % (g, q0))
 
         def quantize_e(g, q0, nq):
-            e_q[g, q0] = quantize(e_bf[g, q0][:].rearrange("p q m t -> p (q m t)"), nq * QUARTER, "e_q%d_%d" % (g, q0))
+            cols = e_bf[g][:, q0 * QUARTER : (q0 + nq) * QUARTER, :]
+            e_q[g, q0] = quantize(cols.rearrange("p m t -> p (m t)"), nq * QUARTER, "e_q%d_%d" % (g, q0))
 
         wm_bf = {}
         wm_q = {}
@@ -247,7 +267,7 @@ def tile_list_permission_drift_features_kernel(
                 y[q] = bank(q, [P, 4, QUARTER], "y_acc%d" % q)
             d_part = (wd_w[:, g, :], 2, FP4X4, wd_s[:, g, :], d_q[g, q0])
             e_part = (wm_q[g][0][:], 1, FP8X4, wm_q[g][1][:], e_q[g, q0])
-            parts = [d_part, e_part] if g == 0 else [e_part, d_part]
+            parts = [e_part, d_part]
             for i, (words, per, fmt, plane, (codes, scales)) in enumerate(parts):
                 for c in range(4):
                     nc.tensor.matmul_mx(
@@ -264,7 +284,7 @@ def tile_list_permission_drift_features_kernel(
 
         def finish(q):
             res = tile([P, 4, QUARTER], F32, "res%d" % q)
-            if q < 2:
+            if q < 3:
                 for c in range(4):
                     nc.scalar.activation(res[:, c, :], y[q][:, c, :], ACT.Identity, bias=bo_t[:, c : c + 1])
             else:
@@ -273,49 +293,53 @@ def tile_list_permission_drift_features_kernel(
 
         for t in range(4):
             make_h(0, t)
+        round_w1(1, 0, nc.vector.tensor_copy)
+        quantize_w1(1, 0)
         for t in range(4):
             make_b(0, t)
-        round_w1(1, 0, nc.vector.tensor_copy)
         round_w1(1, 1, nc.scalar.copy)
-        fetch(0, 0)
-        fetch(0, 1)
-        combine(0, 0)
-        quantize_w1(1, 0)
-        combine(0, 1)
         quantize_w1(1, 1)
-        fetch_pair("w1_bf11")
-        combine(0, 2)
-        combine(0, 3)
-        round_wm(0, "w1_bf00", nc.scalar.copy)
+        bg0 = tile([P, PACK, M], F32, "bg0", "w1_raw11")
+        bg_pair[0, 0], bg_pair[0, 1] = bg0[:, 0:2, :], bg0[:, 2:4, :]
+        scale_b(0, 0)
+        fetch_pair(0, 0)
+        subtract_pair(0, 0)
+        multiply_pair(0, 0)
+        fetch_pair(0, 1, "w1_bf11")
+        subtract_pair(0, 1)
         make_h(1, 0)
         make_h(1, 1)
+        scale_b(0, 1)
+        multiply_pair(0, 1)
         make_b(1, 0)
+        make_b(1, 1)
+        weave_d(0, 0, 4)
+        bg1 = tile([P, PACK, M], F32, "bg1", "w1_raw00")
+        bg_pair[1, 0], bg_pair[1, 1] = bg1[:, 0:2, :], bg1[:, 2:4, :]
+        scale_b(1, 0)
         make_h(1, 2)
         make_h(1, 3)
-        make_b(1, 1)
         make_b_late(0)
         make_b_late(1)
-        weave_d(0, 0, 4, "w1_q11_c")
-        weave_e(0, 0, 4, nc.scalar.copy, "w1_q10_c")
-        round_wm(1, "w1_bf01", nc.scalar.copy)
+        scale_b_late()
+        round_wm(0, "w1_bf00", nc.scalar.copy)
+        round_wm(1, "w1_bf01", nc.vector.tensor_copy)
         quantize_wm(0)
         quantize_d(0, 0, 4)
         quantize_e(0, 0, 4)
         for q in range(4):
             second_stage(0, 0, q)
         quantize_wm(1)
-        fetch(1, 0)
-        fetch(1, 1)
-        combine(1, 0)
-        combine(1, 1)
-        late = [(0, 2, None), (2, 1, "w1_q10_c"), (3, 1, "w1_q10_c")]
+        fetch_pair(1, 0)
+        subtract_pair(1, 0)
+        multiply_pair(1, 0)
+        late = [(0, 2, "d_bf0_0"), (2, 1, "e_bf0"), (3, 1, "e_bf0")]
         for q0, nq, slot in late:
             fetch_late(q0, nq, slot)
             combine_late(q0, nq)
             weave_d(1, q0, nq)
-            weave_e(1, q0, nq, nc.vector.tensor_copy if q0 == 3 else nc.scalar.copy)
-            quantize_e(1, q0, nq)
             quantize_d(1, q0, nq)
+            quantize_e(1, q0, nq)
         for q0, nq, slot in late:
             for q in range(q0, q0 + nq):
                 second_stage(1, q0, q)

from contextlib import ExitStack

import concourse.mybir as mybir

K, H, N, T, S, M = 1024, 1024, 512, 2048, 1024, 512
FLOPS = 2 * K * H * (S + M) + 4 * H * N * M

F32 = mybir.dt.float32
BF16 = mybir.dt.bfloat16
I32 = mybir.dt.int32
U32 = mybir.dt.uint32
U16 = mybir.dt.uint16
U8 = mybir.dt.uint8
FP8X4 = mybir.dt.float8_e4m3fn_x4
FP4X4 = mybir.dt.float4_e2m1fn_x4
ACT = mybir.ActivationFunctionType
ALU = mybir.AluOpType

P = 128
PACK = 4
PASS = 512
BANK = 512
QUARTER = 128


def tile_list_permission_drift_features_kernel(
    tc, tab_words, tab_scales, tab2_words, tab2_scales, offs, pos1, offs2, w1, ge, wd_words, wd_scales, wm, bo, out
):
    nc = tc.nc
    with ExitStack() as ctx:
        lists = ctx.enter_context(tc.tile_pool(name="lists", bufs=1))
        keep = ctx.enter_context(tc.tile_pool(name="keep", bufs=1))
        psum = ctx.enter_context(tc.psum_pool(name="psum", bufs=1))

        def tile(shape, dtype, name, slot=None):
            return keep.tile(shape, dtype, name=name, tag=slot or name, align_bytes=256)

        def bank(index, shape, name):
            return psum.tile(shape, F32, name=name, tag="bank%d" % index)

        offs_t = lists.tile([P, S // 16], U16, name="offs_t")
        offs2_t = lists.tile([P, M // 16], U16, name="offs2_t")
        pos1_t = lists.tile([P, M // 16], U16, name="pos1_t")

        tab_s = tile([P, T], U8, "tab_s")
        tab2_s = tile([P, T], U8, "tab2_s")
        wd_s = tile([P, 2, N], U8, "wd_s")
        nc.vector.memset(tab_s[:].bitcast(I32), 0)
        nc.gpsimd.memset(tab2_s[:].bitcast(I32), 0)
        nc.gpsimd.memset(wd_s[:].bitcast(I32), 0)

        def load_words(queue, words, a, name):
            t = tile([P, T], I32, name)
            queue.dma_start(t[:], words[a].rearrange("p t i -> p (t i)").bitcast(I32))
            return t

        def load_table_scales(queue, plane, scales):
            for q in range(4):
                queue.dma_start(plane[32 * q : 32 * q + 8, :].bitcast(I32), scales[:, 4 * q : 4 * q + 4, :].bitcast(I32))

        def load_rows(src, a, c0, width, name):
            t = tile([P, PACK, width], F32, name)
            nc.sync.dma_start(t[:], src[PASS * a : PASS * (a + 1), c0 : c0 + width].rearrange("(p j) c -> p j c", j=PACK))
            return t

        tab_w = [None, None]
        nc.sync.dma_start(offs_t[:], offs)
        tab_w[0] = load_words(nc.sync, tab_words, 0, "tab_w0")
        nc.sync.dma_start(offs2_t[:], offs2)
        nc.sync.dma_start(pos1_t[:], pos1)
        load_table_scales(nc.sync, tab_s, tab_scales)
        w1_raw = {}
        w1_raw[0, 0] = [load_rows(w1, 0, 0, 512, "w1_raw00")]
        tab_w[1] = load_words(nc.sync, tab_words, 1, "tab_w1")
        w1_raw[0, 1] = [load_rows(w1, 1, 256 * hh, 256, "w1_raw01%d" % hh) for hh in range(2)]
        tab2_w = [None, None]
        load_table_scales(nc.sync, tab2_s, tab2_scales)
        tab2_w[0] = load_words(nc.sync, tab2_words, 0, "tab2_w0")
        ge_t = tile([P, 2, PACK], F32, "ge_t")
        nc.sync.dma_start(ge_t[:], ge.rearrange("(g p t) -> p g t", g=2, t=PACK))
        tab2_w[1] = load_words(nc.sync, tab2_words, 1, "tab2_w1")
        w1_raw[1, 0] = [load_rows(w1, 0, 512, 512, "w1_raw10")]
        w1_raw[1, 1] = [load_rows(w1, 1, 512, 512, "w1_raw11")]
        wm_raw = [load_rows(wm, a, 0, 512, "wm_raw%d" % a) for a in range(2)]
        wd_w = tile([P, 2, 2 * N], U8, "wd_w")
        nc.sync.dma_start(wd_w[:].bitcast(I32), wd_words.rearrange("a p c -> p a c").bitcast(I32))
        for q in range(4):
            nc.sync.dma_start(
                wd_s[32 * q : 32 * q + 4, :, :].bitcast(I32),
                wd_scales[:, 4 * q : 4 * q + 4, :].rearrange("a r n -> r a n").bitcast(I32),
            )
        bo_t = tile([P, 4], F32, "bo_t")
        with nc.allow_non_contiguous_dma(reason="one bias value to a partition"):
            nc.sync.dma_start(bo_t[:], bo.rearrange("(c p) -> p c", p=P))

        def gather(window, offsets, count, dtype, name, slot=None):
            t = tile([P, count], dtype, name, slot)
            nc.vector.tensor_copy(t[:], window.indirect(offsets))
            return t

        def quantize(src, width, name):
            codes = tile([P, width], U32, name + "_c")
            scales = tile([P, width], U8, name + "_s")
            nc.vector.quantize_mx(out=codes[:].bitcast(FP8X4), scales=scales[:], in_=src)
            return codes, scales

        w1_bf = {}
        w1_q = {}

        def round_w1(g, a, copy):
            w1_bf[g, a] = tile([P, PACK, P, PACK], BF16, "w1_bf%d%d" % (g, a))
            pieces = w1_raw[g, a]
            per = P // len(pieces)
            for i, raw in enumerate(pieces):
                copy(
                    w1_bf[g, a][:, :, per * i : per * (i + 1), :].rearrange("p t m j -> p m j t"),
                    raw[:].rearrange("p j (m t) -> p m j t", t=PACK),
                )

        def quantize_w1(g, a):
            w1_q[g, a] = quantize(w1_bf[g, a][:].rearrange("p t m j -> p (t m j)"), PASS, "w1_q%d%d" % (g, a))

        v_w = [None, None]
        v_s = gather(tab_s[:], offs_t[:], S, U8, "v_s")
        v_w[0] = gather(tab_w[0][:].bitcast(U32), offs_t[:], S, U32, "v_w0")
        round_w1(0, 0, nc.scalar.copy)
        v_w[1] = gather(tab_w[1][:].bitcast(U32), offs_t[:], S, U32, "v_w1")
        quantize_w1(0, 0)
        round_w1(0, 1, nc.scalar.copy)
        quantize_w1(0, 1)
        v2_w = [None, None]
        v2_w[0] = gather(tab2_w[0][:].bitcast(U32), offs2_t[:], M, U32, "v2_w0")
        v2_s = gather(tab2_s[:], offs2_t[:], M, U8, "v2_s")
        v2_w[1] = gather(tab2_w[1][:].bitcast(U32), offs2_t[:], M, U32, "v2_w1")

        def project(dst, g, t, words, plane, cols):
            for a in range(2):
                codes, scales = w1_q[g, a]
                nc.tensor.matmul_mx(
                    out=dst,
                    lhsT=codes[:, P * t : P * (t + 1)].bitcast(FP8X4),
                    lhsT_scale=scales[:, P * t : P * (t + 1)],
                    rhs=words[a][:, cols].bitcast(FP8X4),
                    rhs_scale=plane[4 * a : P, cols],
                    start=(a == 0),
                    stop=(a == 1),
                )

        h = {}
        b = {}

        def make_h(g, t):
            h[g, t] = tile([P, S], F32, "h%d%d" % (g, t))
            for half in range(2):
                cols = slice(BANK * half, BANK * (half + 1))
                acc = bank((2 * t + half) % 4, [P, BANK], "h_acc%d%d%d" % (g, t, half))
                project(acc[:], g, t, v_w, v_s, cols)
                nc.scalar.copy(h[g, t][:, cols], acc[:])

        def make_b(g, t):
            b[g, t] = bank(4 + t, [P, M], "b_acc%d%d" % (g, t))
            project(b[g, t][:], g, t, v2_w, v2_s, slice(0, M))

        b_late = {}

        def make_b_late(half):
            b_late[half] = bank(6 + half, [P, 2, M // 2], "b_late%d" % half)
            for i in range(2):
                project(b_late[half][:, i, :], 1, 2 + i, v2_w, v2_s, slice(256 * half, 256 * (half + 1)))

        diff = [tile([P, 4, PACK, QUARTER], BF16, "diff%d" % g) for g in range(2)]
        e_bf = [tile([P, M, PACK], BF16, "e_bf%d" % g) for g in range(2)]
        a_pair, bg_pair = {}, {}

        def fetch_pair(g, tp, slot=None):
            a_pair[g, tp] = tile([P, 2, M], F32, "a%d%d" % (g, tp), slot)
            for i in range(2):
                nc.vector.tensor_copy(a_pair[g, tp][:, i, :], h[g, 2 * tp + i][:].indirect(pos1_t[:]))

        def scale_b(g, tp):
            for i in range(2):
                t = 2 * tp + i
                nc.scalar.activation(bg_pair[g, tp][:, i, :], b[g, t][:], ACT.Copy, scale=ge_t[:, g, t : t + 1])

        def scale_b_late():
            for half in range(2):
                for i in range(2):
                    nc.scalar.activation(
                        bg_pair[1, 1][:, i, 256 * half : 256 * (half + 1)],
                        b_late[half][:, i, :],
                        ACT.Copy,
                        scale=ge_t[:, 1, 2 + i : 3 + i],
                    )

        def subtract_pair(g, tp):
            for i in range(2):
                t = 2 * tp + i
                nc.vector.tensor_tensor(
                    diff[g][:, :, t, :],
                    a_pair[g, tp][:, i, :].rearrange("p (q m) -> p q m", q=4),
                    b[g, t][:].rearrange("p (q m) -> p q m", q=4),
                    ALU.subtract,
                )

        def multiply(g, tp, a_cols, m0, width):
            nc.gpsimd.tensor_tensor(
                e_bf[g][:, m0 : m0 + width, 2 * tp : 2 * tp + 2],
                a_cols.rearrange("p t m -> p m t"),
                bg_pair[g, tp][:, :, m0 : m0 + width].rearrange("p t m -> p m t"),
                ALU.mult,
            )

        def multiply_pair(g, tp):
            for half in range(2):
                multiply(g, tp, a_pair[g, tp][:, :, 256 * half : 256 * (half + 1)], 256 * half, 256)

        a_late = {}

        def fetch_late(q0, nq, slot):
            a_late[q0] = tile([P, 2, nq * QUARTER], F32, "a_late%d" % q0, slot)
            offsets = pos1_t[:, q0 * QUARTER // 16 : (q0 + nq) * QUARTER // 16]
            for i in range(2):
                nc.vector.tensor_copy(a_late[q0][:, i, :], h[1, 2 + i][:].indirect(offsets))

        def combine_late(q0, nq):
            c0 = (q0 % 2) * QUARTER
            a_q = a_late[q0][:].rearrange("p t (q m) -> p t q m", q=nq)
            b_q = b_late[q0 // 2][:, :, c0 : c0 + nq * QUARTER].rearrange("p t (q m) -> p t q m", q=nq)
            nc.vector.tensor_tensor(diff[1][:, q0 : q0 + nq, 2:4, :].rearrange("p q t m -> p t q m"), a_q, b_q, ALU.subtract)
            multiply(1, 1, a_late[q0][:], q0 * QUARTER, nq * QUARTER)

        d_bf, d_q, e_q = {}, {}, {}

        def weave_d(g, q0, nq, slot=None):
            d_bf[g, q0] = tile([P, nq, QUARTER, PACK], BF16, "d_bf%d_%d" % (g, q0), slot)
            for q in range(nq):
                nc.scalar.activation(
                    d_bf[g, q0][:, q].rearrange("p (c i) t -> p c t i", i=4),
                    diff[g][:, q0 + q].rearrange("p t (c i) -> p c t i", i=4),
                    ACT.Abs,
                )

        def quantize_d(g, q0, nq):
            d_q[g, q0] = quantize(d_bf[g, q0][:].rearrange("p q m t -> p (q m t)"), nq * QUARTER, "d_q%d_%d" % (g, q0))

        def quantize_e(g, q0, nq):
            cols = e_bf[g][:, q0 * QUARTER : (q0 + nq) * QUARTER, :]
            e_q[g, q0] = quantize(cols.rearrange("p m t -> p (m t)"), nq * QUARTER, "e_q%d_%d" % (g, q0))

        wm_bf = {}
        wm_q = {}

        def round_wm(a, slot, copy):
            wm_bf[a] = tile([P, N, PACK], BF16, "wm_bf%d" % a, slot)
            copy(
                wm_bf[a][:].rearrange("p (c i) j -> p c j i", i=4), wm_raw[a][:].rearrange("p j (c i) -> p c j i", i=4)
            )

        def quantize_wm(a):
            wm_q[a] = quantize(wm_bf[a][:].rearrange("p n j -> p (n j)"), N, "wm_q%d" % a)

        y = {}

        def second_stage(g, q0, q):
            cols = slice(QUARTER * (q - q0), QUARTER * (q - q0 + 1))
            if g == 0:
                y[q] = bank(q, [P, 4, QUARTER], "y_acc%d" % q)
            d_part = (wd_w[:, g, :], 2, FP4X4, wd_s[:, g, :], d_q[g, q0])
            e_part = (wm_q[g][0][:], 1, FP8X4, wm_q[g][1][:], e_q[g, q0])
            parts = [e_part, d_part]
            for i, (words, per, fmt, plane, (codes, scales)) in enumerate(parts):
                for c in range(4):
                    nc.tensor.matmul_mx(
                        out=y[q][:, c, :],
                        lhsT=words[:, per * P * c : per * P * (c + 1)].bitcast(fmt),
                        lhsT_scale=plane[:, P * c : P * (c + 1)],
                        rhs=codes[:, cols].bitcast(FP8X4),
                        rhs_scale=scales[:, cols],
                        start=(g == 0 and i == 0 and c == 0),
                        stop=(g == 1 and i == 1 and c == 3),
                    )

        out_v = out.rearrange("(c p) m -> p c m", p=P)

        def finish(q):
            res = tile([P, 4, QUARTER], F32, "res%d" % q)
            if q < 3:
                for c in range(4):
                    nc.scalar.activation(res[:, c, :], y[q][:, c, :], ACT.Identity, bias=bo_t[:, c : c + 1])
            else:
                nc.vector.tensor_tensor(res[:], y[q][:], bo_t[:].unsqueeze(2).to_broadcast([P, 4, QUARTER]), ALU.add)
            nc.sync.dma_start(out_v[:, :, QUARTER * q : QUARTER * (q + 1)], res[:])

        for t in range(4):
            make_h(0, t)
        round_w1(1, 0, nc.vector.tensor_copy)
        quantize_w1(1, 0)
        for t in range(4):
            make_b(0, t)
        round_w1(1, 1, nc.scalar.copy)
        quantize_w1(1, 1)
        bg0 = tile([P, PACK, M], F32, "bg0", "w1_raw11")
        bg_pair[0, 0], bg_pair[0, 1] = bg0[:, 0:2, :], bg0[:, 2:4, :]
        scale_b(0, 0)
        fetch_pair(0, 0)
        subtract_pair(0, 0)
        multiply_pair(0, 0)
        fetch_pair(0, 1, "w1_bf11")
        subtract_pair(0, 1)
        make_h(1, 0)
        make_h(1, 1)
        scale_b(0, 1)
        multiply_pair(0, 1)
        make_b(1, 0)
        make_b(1, 1)
        weave_d(0, 0, 4)
        bg1 = tile([P, PACK, M], F32, "bg1", "w1_raw00")
        bg_pair[1, 0], bg_pair[1, 1] = bg1[:, 0:2, :], bg1[:, 2:4, :]
        scale_b(1, 0)
        make_h(1, 2)
        make_h(1, 3)
        make_b_late(0)
        make_b_late(1)
        scale_b_late()
        round_wm(0, "w1_bf00", nc.scalar.copy)
        round_wm(1, "w1_bf01", nc.vector.tensor_copy)
        quantize_wm(0)
        quantize_d(0, 0, 4)
        quantize_e(0, 0, 4)
        for q in range(4):
            second_stage(0, 0, q)
        quantize_wm(1)
        fetch_pair(1, 0)
        subtract_pair(1, 0)
        multiply_pair(1, 0)
        late = [(0, 2, "d_bf0_0"), (2, 1, "e_bf0"), (3, 1, "e_bf0")]
        for q0, nq, slot in late:
            fetch_late(q0, nq, slot)
            combine_late(q0, nq)
            weave_d(1, q0, nq)
            quantize_d(1, q0, nq)
            quantize_e(1, q0, nq)
        for q0, nq, slot in late:
            for q in range(q0, q0 + nq):
                second_stage(1, q0, q)
                finish(q)
